import numpy as np
import ml_dtypes


def mxq(x, axis, fmt="e4m3"):
    dtype, down = {"e4m3": (ml_dtypes.float8_e4m3fn, 7), "e5m2": (ml_dtypes.float8_e5m2, 14)}[fmt]
    v = np.moveaxis(np.asarray(x, np.float32).astype(ml_dtypes.bfloat16).astype(np.float64), axis, -1)
    blocks = v.reshape(v.shape[:-1] + (-1, 32))
    amax = np.abs(blocks).max(-1, keepdims=True)
    byte = np.maximum(np.where(amax > 0, np.frexp(amax)[1] - 1 + 127, 0) - down, 1)
    scale = np.exp2(byte - 127.0)
    codes = (blocks / scale).astype(np.float32).astype(dtype).astype(np.float64)
    return np.moveaxis((codes * scale).reshape(v.shape), -1, axis)


WIDE = False


def mx_kscale(k):
    if not WIDE:
        return np.ones(k)
    levels = np.array([10, -10, 5, -5, 0])
    if k % 512:
        return np.exp2(np.random.permutation(np.resize(levels, k // 32))).repeat(32)
    a = np.empty((k // 512, 16))
    for p in range(k // 512):
        a[p, :8] = np.random.permutation(np.resize(levels, 8))
        for g in range(8):
            far = levels[np.abs(levels - a[p, g]) >= 10]
            a[p, g + 8] = far[np.random.randint(len(far))]
    return np.exp2(a.ravel()).repeat(32)


def f64(x):
    return np.asarray(x).astype(np.float64)


def striped8(idx):
    return np.concatenate([v.reshape(-1, 16).T for v in idx]).astype(np.uint16)


def unstriped8(offs):
    return np.stack([offs[16 * g:16 * g + 16].T.reshape(-1) for g in range(8)]).astype(np.int64)


E2M1 = np.array([0.0, 0.5, 1.0, 1.5, 2.0, 3.0, 4.0, 6.0, -0.0, -0.5, -1.0, -1.5, -2.0, -3.0, -4.0, -6.0])


def pack_weight(w, fmt):
    k, n = w.shape
    w = f64(np.asarray(w, np.float32).astype(ml_dtypes.bfloat16)).reshape(k // 32, 32, n)
    amax = np.abs(w).max(1)
    if fmt == "e4m3":
        byte = np.frexp(amax)[1] - 1 + 127 - 7
    else:
        mant, ex = np.frexp(amax / 6.0)
        byte = np.where(mant > 0.5, ex, ex - 1) + 127
    byte = np.clip(np.where(amax > 0, byte, 1), 1, 254)
    scaled = (w * np.exp2(127.0 - byte)[:, None, :]).reshape(k, n).astype(np.float32)
    by_word = np.ascontiguousarray(scaled.reshape(k // 512, 128, 4, n).transpose(0, 1, 3, 2))
    if fmt == "e4m3":
        words = by_word.astype(ml_dtypes.float8_e4m3fn).view(np.uint8)
    else:
        c = by_word.astype(ml_dtypes.float4_e2m1fn).view(np.uint8) & 0xF
        words = (c[..., 0::2] | (c[..., 1::2] << 4)).reshape(k // 512, 128, 2 * n)
    return np.ascontiguousarray(words), np.ascontiguousarray(byte.astype(np.uint8).reshape(k // 512, 16, n))


def unpack_weight(words, scales, fmt):
    g, _, n = scales.shape
    words = np.ascontiguousarray(words).reshape(g, 128, n, -1)
    if fmt == "e4m3":
        vals = words.view(ml_dtypes.float8_e4m3fn).astype(np.float64)
    else:
        nib = np.empty((g, 128, n, 4), np.uint8)
        nib[..., 0::2] = words & 0xF
        nib[..., 1::2] = words >> 4
        vals = E2M1[nib]
    vals = vals * np.repeat(np.exp2(scales.astype(np.float64) - 127.0), 8, axis=1)[..., None]
    return vals.transpose(0, 1, 3, 2).reshape(g * 512, n)


K, M, T, S = 2048, 256, 512, 256


def setup_inputs():
    n = np.random.standard_normal
    s = mx_kscale(K)[:, None]
    u = mx_kscale(512)[:, None]
    p_w2 = pack_weight(1.4 * n((512, M)) / np.sqrt(512) / u, "e2m1")
    return {
        "x": (n((K, S)) * s).astype(np.float32),
        "w1": (n((K, 512)) / np.sqrt(K) / s * u.T).astype(np.float32),
        "w2_words": p_w2[0],
        "w2_scales": p_w2[1],
        "b": (0.3 * n(256)).astype(np.float32),
        "wgo": np.repeat(np.random.uniform(0.5, 2.0, (8, S)), 16, axis=0).astype(np.float32),
        "offs": striped8(np.stack([np.random.permutation(T)[:S] for _ in range(8)])),
    }


def reference(x, w1, w2_words, w2_scales, b, wgo, offs):
    x_ = mxq(f64(x), 0, "e4m3")
    w1_ = mxq(f64(w1), 0, "e4m3")
    w2_ = unpack_weight(w2_words, w2_scales, "e2m1")
    h_ = mxq(np.maximum(w1_.T @ x_, 0.0), 0, "e4m3")
    y = w2_.T @ h_
    place = unstriped8(offs)[np.arange(M) % 128 // 16]
    out = np.zeros((M, T))
    out[np.arange(M)[:, None], place] = f64(wgo)[np.arange(M) % 128] * (y + f64(b)[:, None])
    return out

@@ -1,0 +1,198 @@
+from contextlib import ExitStack
+
+import concourse.mybir as mybir
+
+K, H, M, T, S = 2048, 512, 256, 512, 256
+FLOPS = 2 * K * H * S + 2 * H * M * S
+
+F32 = mybir.dt.float32
+BF16 = mybir.dt.bfloat16
+I32 = mybir.dt.int32
+U32 = mybir.dt.uint32
+U16 = mybir.dt.uint16
+U8 = mybir.dt.uint8
+FP8X4 = mybir.dt.float8_e4m3fn_x4
+FP4X4 = mybir.dt.float4_e2m1fn_x4
+ACT = mybir.ActivationFunctionType
+MULT = mybir.AluOpType.mult
+
+P = 128
+PACK = 4
+PASSES = K // (P * PACK)
+HALF = S // 2
+BLOCKS = M // P
+
+
+def tile_list_hscat_m_bias_kernel(tc, x, w1, w2_words, w2_scales, b, wgo, offs, out):
+    nc = tc.nc
+    with ExitStack() as ctx:
+        sb = ctx.enter_context(tc.tile_pool(name="sb", bufs=1))
+        ps = ctx.enter_context(tc.psum_pool(name="ps", bufs=1))
+
+        def tile(shape, dtype, name):
+            return sb.tile(shape, dtype, name=name, align_bytes=64)
+
+        def copy(engine, dst, src):
+            if engine == "scalar":
+                nc.scalar.copy(out=dst, in_=src)
+            else:
+                nc.vector.tensor_copy(out=dst, in_=src)
+
+        offsets = tile([P, S // 16], U16, "offsets")
+        w_raw = [tile([P, PACK, H], F32, "w_raw%d" % a) for a in range(PASSES)]
+        x_raw = {(h, a): tile([P, PACK, HALF], F32, "x_raw%d%d" % (h, a)) for h in range(2) for a in range(PASSES)}
+        w2_codes = tile([P, 2 * M], U8, "w2_codes")
+        w2_plane = tile([P, M], U8, "w2_plane")
+        bias = tile([P, BLOCKS], F32, "bias")
+        weights = tile([P, S], F32, "weights")
+        pages = [tile([P, T], F32, "page%d" % c) for c in range(BLOCKS)]
+
+        def load_w1(a):
+            nc.sync.dma_start(out=w_raw[a][:], in_=w1[512 * a : 512 * (a + 1), :].rearrange("(p j) r -> p j r", j=PACK))
+
+        def load_x(h, a):
+            rows = x[512 * a : 512 * (a + 1), HALF * h : HALF * (h + 1)]
+            nc.sync.dma_start(out=x_raw[h, a][:], in_=rows.rearrange("(p j) s -> p j s", j=PACK))
+
+        nc.vector.memset(w2_plane[:].bitcast(I32), 0)
+        load_w1(0)
+        load_w1(1)
+        nc.sync.dma_start(offsets[:], offs)
+        with nc.allow_non_contiguous_dma(reason="one bias value for each partition"):
+            nc.sync.dma_start(out=bias[:], in_=b.rearrange("(c p) -> p c", p=P))
+        for q in range(4):
+            nc.sync.dma_start(
+                out=w2_plane[32 * q : 32 * q + 4, :].bitcast(I32), in_=w2_scales[0, 4 * q : 4 * q + 4, :].bitcast(I32)
+            )
+        load_w1(2)
+        load_w1(3)
+        nc.sync.dma_start(out=w2_codes[:].bitcast(I32), in_=w2_words[0].bitcast(I32))
+        for h in range(2):
+            for a in range(PASSES):
+                load_x(h, a)
+        nc.sync.dma_start(out=weights[:], in_=wgo)
+
+        for page in pages:
+            nc.vector.memset(page[:], 0.0)
+
+        w_bf = {}
+        w_q = {}
+        x_bf = {}
+        x_q = {}
+
+        def cast_w1(a, u, engine):
+            w_bf[a, u] = tile([P, 2, P, PACK], BF16, "w_bf%d%d" % (a, u))
+            src = w_raw[a][:].rearrange("p j (m t) -> p m j t", t=PACK)[:, :, :, 2 * u : 2 * u + 2]
+            copy(engine, w_bf[a, u][:].rearrange("p t m j -> p m j t"), src)
+
+        def quantize(src, columns, name):
+            codes = tile([P, columns], U32, name + "_codes")
+            plane = tile([P, columns], U8, name + "_plane")
+            nc.vector.quantize_mx(out=codes[:].bitcast(FP8X4), scales=plane[:], in_=src)
+            return codes, plane
+
+        def quant_w1(a, u):
+            w_q[a, u] = quantize(w_bf[a, u][:].rearrange("p t m j -> p (t m j)"), 2 * P, "w%d%d" % (a, u))
+
+        def cast_x(h, a, engine):
+            x_bf[h, a] = tile([P, HALF, PACK], BF16, "x_bf%d%d" % (h, a))
+            copy(
+                engine,
+                x_bf[h, a][:].rearrange("p (c i) j -> p c j i", i=4),
+                x_raw[h, a][:].rearrange("p j (c i) -> p c j i", i=4),
+            )
+
+        def quant_x(h, a):
+            x_q[h, a] = quantize(x_bf[h, a][:].rearrange("p s j -> p (s j)"), HALF, "x%d%d" % (h, a))
+
+        h_acc = [ps.tile([P, PACK, HALF], F32, name="h_acc%d" % h) for h in range(2)]
+
+        def first_product(h, a):
+            x_codes, x_plane = x_q[h, a]
+            for t in range(PACK):
+                w_codes, w_plane = w_q[a, t // 2]
+                cols = slice(P * (t % 2), P * (t % 2 + 1))
+                nc.tensor.matmul_mx(
+                    out=h_acc[h][:, t, :],
+                    lhsT=w_codes[:, cols].bitcast(FP8X4),
+                    lhsT_scale=w_plane[:, cols],
+                    rhs=x_codes[:].bitcast(FP8X4),
+                    rhs_scale=x_plane[:],
+                    start=(a == 0 and t == 0),
+                    stop=(a == PASSES - 1 and t == PACK - 1),
+                )
+
+        h_bf = {}
+        h_q = {}
+        y = {}
+
+        def relu(h):
+            h_bf[h] = tile([P, HALF, PACK], BF16, "h_bf%d" % h)
+            nc.scalar.activation(out=h_bf[h][:], in_=h_acc[h][:].rearrange("p t s -> p s t"), func=ACT.Relu)
+
+        def quant_h(h):
+            h_q[h] = quantize(h_bf[h][:].rearrange("p s t -> p (s t)"), HALF, "h%d" % h)
+
+        def second_product(h):
+            h_codes, h_plane = h_q[h]
+            for c in range(BLOCKS):
+                acc = ps.tile([P, HALF], F32, name="y_acc%d%d" % (h, c))
+                nc.tensor.matmul_mx(
+                    out=acc[:],
+                    lhsT=w2_codes[:, 2 * P * c : 2 * P * (c + 1)].bitcast(FP4X4),
+                    lhsT_scale=w2_plane[:, P * c : P * (c + 1)],
+                    rhs=h_codes[:].bitcast(FP8X4),
+                    rhs_scale=h_plane[:],
+                    start=True,
+                    stop=True,
+                )
+                y[h, c] = tile([P, HALF], F32, "y%d%d" % (h, c))
+                nc.scalar.activation(out=y[h, c][:], in_=acc[:], func=ACT.Identity, bias=bias[:, c : c + 1])
+
+        def scatter(h, c):
+            window = pages[c][:].indirect(offsets[:, 8 * h : 8 * (h + 1)])
+            nc.vector.tensor_tensor(window, y[h, c][:], weights[:, HALF * h : HALF * (h + 1)], MULT)
+
+        for a in range(PASSES):
+            cast_w1(a, 0, "scalar")
+            cast_w1(a, 1, "vector")
+            if a < PASSES - 1:
+                quant_w1(a, 1)
+                quant_w1(a, 0)
+        cast_x(0, 0, "vector")
+        quant_w1(3, 1)
+        quant_x(0, 0)
+        quant_w1(3, 0)
+        first_product(0, 0)
+        cast_x(0, 1, "scalar")
+        quant_x(0, 1)
+        first_product(0, 1)
+        cast_x(0, 2, "scalar")
+        cast_x(0, 3, "vector")
+        quant_x(0, 2)
+        quant_x(0, 3)
+        first_product(0, 2)
+        first_product(0, 3)
+        cast_x(1, 0, "scalar")
+        relu(0)
+        cast_x(1, 1, "vector")
+        quant_x(1, 0)
+        first_product(1, 0)
+        cast_x(1, 2, "vector")
+        quant_x(1, 1)
+        first_product(1, 1)
+        quant_x(1, 2)
+        first_product(1, 2)
+        cast_x(1, 3, "vector")
+        quant_h(0)
+        quant_x(1, 3)
+        second_product(0)
+        first_product(1, 3)
+        relu(1)
+        scatter(0, 0)
+        quant_h(1)
+        scatter(0, 1)
+        second_product(1)
+        for c in range(BLOCKS):
+            scatter(1, c)
+            nc.sync.dma_start(out=out[P * c : P * (c + 1), :], in_=pages[c][:])

@@ -29,8 +29,8 @@ def tile_list_hscat_m_bias_kernel(tc, x, w1, w2_words, w2_scales, b, wgo, offs, 
         sb = ctx.enter_context(tc.tile_pool(name="sb", bufs=1))
         ps = ctx.enter_context(tc.psum_pool(name="ps", bufs=1))
 
-        def tile(shape, dtype, name):
-            return sb.tile(shape, dtype, name=name, align_bytes=64)
+        def tile(shape, dtype, name, tag=None):
+            return sb.tile(shape, dtype, name=name, tag=tag or name, align_bytes=64)
 
         def copy(engine, dst, src):
             if engine == "scalar":
@@ -39,38 +39,49 @@ def tile_list_hscat_m_bias_kernel(tc, x, w1, w2_words, w2_scales, b, wgo, offs, 
                 nc.vector.tensor_copy(out=dst, in_=src)
 
         offsets = tile([P, S // 16], U16, "offsets")
-        w_raw = [tile([P, PACK, H], F32, "w_raw%d" % a) for a in range(PASSES)]
+        w_raw = {}
         x_raw = {(h, a): tile([P, PACK, HALF], F32, "x_raw%d%d" % (h, a)) for h in range(2) for a in range(PASSES)}
-        w2_codes = tile([P, 2 * M], U8, "w2_codes")
+        w2_codes = [tile([P, 2 * P], U8, "w2_codes%d" % c) for c in range(BLOCKS)]
         w2_plane = tile([P, M], U8, "w2_plane")
         bias = tile([P, BLOCKS], F32, "bias")
-        weights = tile([P, S], F32, "weights")
+        weights = [tile([P, HALF], F32, "weights%d" % h) for h in range(2)]
         pages = [tile([P, T], F32, "page%d" % c) for c in range(BLOCKS)]
 
-        def load_w1(a):
-            nc.sync.dma_start(out=w_raw[a][:], in_=w1[512 * a : 512 * (a + 1), :].rearrange("(p j) r -> p j r", j=PACK))
+        def load_w1(a, c, parts):
+            width = H // parts
+            w_raw[a, c] = tile([P, PACK, width], F32, "w_raw%d%d" % (a, c))
+            rows = w1[512 * a : 512 * (a + 1), width * c : width * (c + 1)]
+            nc.sync.dma_start(out=w_raw[a, c][:], in_=rows.rearrange("(p j) r -> p j r", j=PACK))
+
+        def load_w2(c):
+            words = w2_words[0, :, 2 * P * c : 2 * P * (c + 1)]
+            nc.sync.dma_start(out=w2_codes[c][:].bitcast(I32), in_=words.bitcast(I32))
 
         def load_x(h, a):
             rows = x[512 * a : 512 * (a + 1), HALF * h : HALF * (h + 1)]
             nc.sync.dma_start(out=x_raw[h, a][:], in_=rows.rearrange("(p j) s -> p j s", j=PACK))
 
         nc.vector.memset(w2_plane[:].bitcast(I32), 0)
-        load_w1(0)
-        load_w1(1)
+        load_w1(0, 0, 1)
+        load_w1(1, 0, 1)
         nc.sync.dma_start(offsets[:], offs)
-        with nc.allow_non_contiguous_dma(reason="one bias value for each partition"):
-            nc.sync.dma_start(out=bias[:], in_=b.rearrange("(c p) -> p c", p=P))
-        for q in range(4):
-            nc.sync.dma_start(
-                out=w2_plane[32 * q : 32 * q + 4, :].bitcast(I32), in_=w2_scales[0, 4 * q : 4 * q + 4, :].bitcast(I32)
-            )
-        load_w1(2)
-        load_w1(3)
-        nc.sync.dma_start(out=w2_codes[:].bitcast(I32), in_=w2_words[0].bitcast(I32))
+        load_w1(2, 0, 1)
+        load_w1(3, 0, 2)
+        load_w1(3, 1, 2)
         for h in range(2):
             for a in range(PASSES):
                 load_x(h, a)
-        nc.sync.dma_start(out=weights[:], in_=wgo)
+            if h == 0:
+                load_w2(0)
+        for h in (1, 0):
+            nc.sync.dma_start(out=weights[h][:], in_=wgo[:, HALF * h : HALF * (h + 1)])
+        load_w2(1)
+        for q in range(4):
+            nc.gpsimd.dma_start(
+                out=w2_plane[32 * q : 32 * q + 4, :].bitcast(I32), in_=w2_scales[0, 4 * q : 4 * q + 4, :].bitcast(I32)
+            )
+        with nc.allow_non_contiguous_dma(reason="one bias value for each partition"):
+            nc.gpsimd.dma_start(out=bias[:], in_=b.rearrange("(c p) -> p c", p=P))
 
         for page in pages:
             nc.vector.memset(page[:], 0.0)
@@ -80,10 +91,13 @@ def tile_list_hscat_m_bias_kernel(tc, x, w1, w2_words, w2_scales, b, wgo, offs, 
         x_bf = {}
         x_q = {}
 
-        def cast_w1(a, u, engine):
-            w_bf[a, u] = tile([P, 2, P, PACK], BF16, "w_bf%d%d" % (a, u))
-            src = w_raw[a][:].rearrange("p j (m t) -> p m j t", t=PACK)[:, :, :, 2 * u : 2 * u + 2]
-            copy(engine, w_bf[a, u][:].rearrange("p t m j -> p m j t"), src)
+        def cast_w1(a, u, c, parts, engine):
+            if c == 0:
+                w_bf[a, u] = tile([P, 2, P, PACK], BF16, "w_bf%d%d" % (a, u))
+            width = P // parts
+            src = w_raw[a, c][:].rearrange("p j (m t) -> p m j t", t=PACK)[:, :, :, 2 * u : 2 * u + 2]
+            dst = w_bf[a, u][:, :, width * c : width * (c + 1), :]
+            copy(engine, dst.rearrange("p t m j -> p m j t"), src)
 
         def quantize(src, columns, name):
             codes = tile([P, columns], U32, name + "_codes")
@@ -124,58 +138,59 @@ def tile_list_hscat_m_bias_kernel(tc, x, w1, w2_words, w2_scales, b, wgo, offs, 
 
         h_bf = {}
         h_q = {}
+        y_acc = {}
         y = {}
 
         def relu(h):
-            h_bf[h] = tile([P, HALF, PACK], BF16, "h_bf%d" % h)
+            h_bf[h] = tile([P, HALF, PACK], BF16, "h_bf%d" % h, "x_raw11" if h == 0 else None)
             nc.scalar.activation(out=h_bf[h][:], in_=h_acc[h][:].rearrange("p t s -> p s t"), func=ACT.Relu)
 
         def quant_h(h):
             h_q[h] = quantize(h_bf[h][:].rearrange("p s t -> p (s t)"), HALF, "h%d" % h)
 
-        def second_product(h):
+        def second_product(h, c):
             h_codes, h_plane = h_q[h]
-            for c in range(BLOCKS):
-                acc = ps.tile([P, HALF], F32, name="y_acc%d%d" % (h, c))
-                nc.tensor.matmul_mx(
-                    out=acc[:],
-                    lhsT=w2_codes[:, 2 * P * c : 2 * P * (c + 1)].bitcast(FP4X4),
-                    lhsT_scale=w2_plane[:, P * c : P * (c + 1)],
-                    rhs=h_codes[:].bitcast(FP8X4),
-                    rhs_scale=h_plane[:],
-                    start=True,
-                    stop=True,
-                )
-                y[h, c] = tile([P, HALF], F32, "y%d%d" % (h, c))
-                nc.scalar.activation(out=y[h, c][:], in_=acc[:], func=ACT.Identity, bias=bias[:, c : c + 1])
+            y_acc[h, c] = ps.tile([P, HALF], F32, name="y_acc%d%d" % (h, c))
+            nc.tensor.matmul_mx(
+                out=y_acc[h, c][:],
+                lhsT=w2_codes[c][:].bitcast(FP4X4),
+                lhsT_scale=w2_plane[:, P * c : P * (c + 1)],
+                rhs=h_codes[:].bitcast(FP8X4),
+                rhs_scale=h_plane[:],
+                start=True,
+                stop=True,
+            )
+
+        def add_bias(h, c):
+            y[h, c] = tile([P, HALF], F32, "y%d%d" % (h, c))
+            nc.scalar.activation(out=y[h, c][:], in_=y_acc[h, c][:], func=ACT.Identity, bias=bias[:, c : c + 1])
 
         def scatter(h, c):
             window = pages[c][:].indirect(offsets[:, 8 * h : 8 * (h + 1)])
-            nc.vector.tensor_tensor(window, y[h, c][:], weights[:, HALF * h : HALF * (h + 1)], MULT)
+            nc.vector.tensor_tensor(window, y[h, c][:], weights[h][:], MULT)
 
-        for a in range(PASSES):
-            cast_w1(a, 0, "scalar")
-            cast_w1(a, 1, "vector")
-            if a < PASSES - 1:
-                quant_w1(a, 1)
-                quant_w1(a, 0)
-        cast_x(0, 0, "vector")
+        for a in range(PASSES - 1):
+            cast_w1(a, 0, 0, 1, "scalar")
+            cast_w1(a, 1, 0, 1, "vector")
+            quant_w1(a, 1)
+            quant_w1(a, 0)
+        for c in range(2):
+            cast_w1(3, 0, c, 2, "scalar")
+            cast_w1(3, 1, c, 2, "vector")
         quant_w1(3, 1)
-        quant_x(0, 0)
         quant_w1(3, 0)
-        first_product(0, 0)
-        cast_x(0, 1, "scalar")
-        quant_x(0, 1)
-        first_product(0, 1)
-        cast_x(0, 2, "scalar")
+        for a in range(3):
+            cast_x(0, a, "scalar")
+        for a in range(2):
+            quant_x(0, a)
+            first_product(0, a)
         cast_x(0, 3, "vector")
-        quant_x(0, 2)
-        quant_x(0, 3)
-        first_product(0, 2)
-        first_product(0, 3)
+        for a in range(2, 4):
+            quant_x(0, a)
+            first_product(0, a)
         cast_x(1, 0, "scalar")
+        cast_x(1, 1, "scalar")
         relu(0)
-        cast_x(1, 1, "vector")
         quant_x(1, 0)
         first_product(1, 0)
         cast_x(1, 2, "vector")
@@ -186,13 +201,18 @@ def tile_list_hscat_m_bias_kernel(tc, x, w1, w2_words, w2_scales, b, wgo, offs, 
         cast_x(1, 3, "vector")
         quant_h(0)
         quant_x(1, 3)
-        second_product(0)
+        second_product(0, 0)
         first_product(1, 3)
+        second_product(0, 1)
+        add_bias(0, 0)
         relu(1)
+        add_bias(0, 1)
         scatter(0, 0)
         quant_h(1)
         scatter(0, 1)
-        second_product(1)
+        for c in range(BLOCKS):
+            second_product(1, c)
+            add_bias(1, c)
         for c in range(BLOCKS):
             scatter(1, c)
             nc.sync.dma_start(out=out[P * c : P * (c + 1), :], in_=pages[c][:])

@@ -44,7 +44,7 @@ def tile_list_hscat_m_bias_kernel(tc, x, w1, w2_words, w2_scales, b, wgo, offs, 
         w2_codes = [tile([P, 2 * P], U8, "w2_codes%d" % c) for c in range(BLOCKS)]
         w2_plane = tile([P, M], U8, "w2_plane")
         bias = tile([P, BLOCKS], F32, "bias")
-        weights = [tile([P, HALF], F32, "weights%d" % h) for h in range(2)]
+        weights = tile([P, S], F32, "weights")
         pages = [tile([P, T], F32, "page%d" % c) for c in range(BLOCKS)]
 
         def load_w1(a, c, parts):
@@ -62,9 +62,15 @@ def tile_list_hscat_m_bias_kernel(tc, x, w1, w2_words, w2_scales, b, wgo, offs, 
             nc.sync.dma_start(out=x_raw[h, a][:], in_=rows.rearrange("(p j) s -> p j s", j=PACK))
 
         nc.vector.memset(w2_plane[:].bitcast(I32), 0)
+        for q in range(4):
+            nc.scalar.dma_start(
+                out=w2_plane[32 * q : 32 * q + 4, :].bitcast(I32), in_=w2_scales[0, 4 * q : 4 * q + 4, :].bitcast(I32)
+            )
+        with nc.allow_non_contiguous_dma(reason="one bias value for each partition"):
+            nc.scalar.dma_start(out=bias[:], in_=b.rearrange("(c p) -> p c", p=P))
+
         load_w1(0, 0, 1)
         load_w1(1, 0, 1)
-        nc.sync.dma_start(offsets[:], offs)
         load_w1(2, 0, 1)
         load_w1(3, 0, 2)
         load_w1(3, 1, 2)
@@ -73,16 +79,9 @@ def tile_list_hscat_m_bias_kernel(tc, x, w1, w2_words, w2_scales, b, wgo, offs, 
                 load_x(h, a)
             if h == 0:
                 load_w2(0)
-        for h in (1, 0):
-            nc.sync.dma_start(out=weights[h][:], in_=wgo[:, HALF * h : HALF * (h + 1)])
+        nc.sync.dma_start(offsets[:], offs)
+        nc.sync.dma_start(out=weights[:], in_=wgo)
         load_w2(1)
-        for q in range(4):
-            nc.gpsimd.dma_start(
-                out=w2_plane[32 * q : 32 * q + 4, :].bitcast(I32), in_=w2_scales[0, 4 * q : 4 * q + 4, :].bitcast(I32)
-            )
-        with nc.allow_non_contiguous_dma(reason="one bias value for each partition"):
-            nc.gpsimd.dma_start(out=bias[:], in_=b.rearrange("(c p) -> p c", p=P))
-
         for page in pages:
             nc.vector.memset(page[:], 0.0)
 
@@ -95,9 +94,9 @@ def tile_list_hscat_m_bias_kernel(tc, x, w1, w2_words, w2_scales, b, wgo, offs, 
             if c == 0:
                 w_bf[a, u] = tile([P, 2, P, PACK], BF16, "w_bf%d%d" % (a, u))
             width = P // parts
-            src = w_raw[a, c][:].rearrange("p j (m t) -> p m j t", t=PACK)[:, :, :, 2 * u : 2 * u + 2]
+            src = w_raw[a, c][:].rearrange("p j (m t) -> p m t j", t=PACK)[:, :, 2 * u : 2 * u + 2, :]
             dst = w_bf[a, u][:, :, width * c : width * (c + 1), :]
-            copy(engine, dst.rearrange("p t m j -> p m j t"), src)
+            copy(engine, dst.rearrange("p t m j -> p m t j"), src)
 
         def quantize(src, columns, name):
             codes = tile([P, columns], U32, name + "_codes")
@@ -167,7 +166,7 @@ def tile_list_hscat_m_bias_kernel(tc, x, w1, w2_words, w2_scales, b, wgo, offs, 
 
         def scatter(h, c):
             window = pages[c][:].indirect(offsets[:, 8 * h : 8 * (h + 1)])
-            nc.vector.tensor_tensor(window, y[h, c][:], weights[h][:], MULT)
+            nc.vector.tensor_tensor(window, y[h, c][:], weights[:, HALF * h : HALF * (h + 1)], MULT)
 
         for a in range(PASSES - 1):
             cast_w1(a, 0, 0, 1, "scalar")

from contextlib import ExitStack

import concourse.mybir as mybir

K, H, M, T, S = 2048, 512, 256, 512, 256
FLOPS = 2 * K * H * S + 2 * H * M * S

F32 = mybir.dt.float32
BF16 = mybir.dt.bfloat16
I32 = mybir.dt.int32
U32 = mybir.dt.uint32
U16 = mybir.dt.uint16
U8 = mybir.dt.uint8
FP8X4 = mybir.dt.float8_e4m3fn_x4
FP4X4 = mybir.dt.float4_e2m1fn_x4
ACT = mybir.ActivationFunctionType
MULT = mybir.AluOpType.mult

P = 128
PACK = 4
PASSES = K // (P * PACK)
HALF = S // 2
BLOCKS = M // P


def tile_list_hscat_m_bias_kernel(tc, x, w1, w2_words, w2_scales, b, wgo, offs, out):
    nc = tc.nc
    with ExitStack() as ctx:
        sb = ctx.enter_context(tc.tile_pool(name="sb", bufs=1))
        ps = ctx.enter_context(tc.psum_pool(name="ps", bufs=1))

        def tile(shape, dtype, name, tag=None):
            return sb.tile(shape, dtype, name=name, tag=tag or name, align_bytes=64)

        def copy(engine, dst, src):
            if engine == "scalar":
                nc.scalar.copy(out=dst, in_=src)
            else:
                nc.vector.tensor_copy(out=dst, in_=src)

        offsets = tile([P, S // 16], U16, "offsets")
        w_raw = {}
        x_raw = {(h, a): tile([P, PACK, HALF], F32, "x_raw%d%d" % (h, a)) for h in range(2) for a in range(PASSES)}
        w2_codes = [tile([P, 2 * P], U8, "w2_codes%d" % c) for c in range(BLOCKS)]
        w2_plane = tile([P, M], U8, "w2_plane")
        bias = tile([P, BLOCKS], F32, "bias")
        weights = tile([P, S], F32, "weights")
        pages = [tile([P, T], F32, "page%d" % c) for c in range(BLOCKS)]

        def load_w1(a, c, parts):
            width = H // parts
            w_raw[a, c] = tile([P, PACK, width], F32, "w_raw%d%d" % (a, c))
            rows = w1[512 * a : 512 * (a + 1), width * c : width * (c + 1)]
            nc.sync.dma_start(out=w_raw[a, c][:], in_=rows.rearrange("(p j) r -> p j r", j=PACK))

        def load_w2(c):
            words = w2_words[0, :, 2 * P * c : 2 * P * (c + 1)]
            nc.sync.dma_start(out=w2_codes[c][:].bitcast(I32), in_=words.bitcast(I32))

        def load_x(h, a):
            rows = x[512 * a : 512 * (a + 1), HALF * h : HALF * (h + 1)]
            nc.sync.dma_start(out=x_raw[h, a][:], in_=rows.rearrange("(p j) s -> p j s", j=PACK))

        nc.vector.memset(w2_plane[:].bitcast(I32), 0)
        for q in range(4):
            nc.scalar.dma_start(
                out=w2_plane[32 * q : 32 * q + 4, :].bitcast(I32), in_=w2_scales[0, 4 * q : 4 * q + 4, :].bitcast(I32)
            )
        with nc.allow_non_contiguous_dma(reason="one bias value for each partition"):
            nc.scalar.dma_start(out=bias[:], in_=b.rearrange("(c p) -> p c", p=P))

        load_w1(0, 0, 1)
        load_w1(1, 0, 1)
        load_w1(2, 0, 1)
        load_w1(3, 0, 2)
        load_w1(3, 1, 2)
        for h in range(2):
            for a in range(PASSES):
                load_x(h, a)
            if h == 0:
                load_w2(0)
        nc.sync.dma_start(offsets[:], offs)
        nc.sync.dma_start(out=weights[:], in_=wgo)
        load_w2(1)
        for page in pages:
            nc.vector.memset(page[:], 0.0)

        w_bf = {}
        w_q = {}
        x_bf = {}
        x_q = {}

        def cast_w1(a, u, c, parts, engine):
            if c == 0:
                w_bf[a, u] = tile([P, 2, P, PACK], BF16, "w_bf%d%d" % (a, u))
            width = P // parts
            src = w_raw[a, c][:].rearrange("p j (m t) -> p m t j", t=PACK)[:, :, 2 * u : 2 * u + 2, :]
            dst = w_bf[a, u][:, :, width * c : width * (c + 1), :]
            copy(engine, dst.rearrange("p t m j -> p m t j"), src)

        def quantize(src, columns, name):
            codes = tile([P, columns], U32, name + "_codes")
            plane = tile([P, columns], U8, name + "_plane")
            nc.vector.quantize_mx(out=codes[:].bitcast(FP8X4), scales=plane[:], in_=src)
            return codes, plane

        def quant_w1(a, u):
            w_q[a, u] = quantize(w_bf[a, u][:].rearrange("p t m j -> p (t m j)"), 2 * P, "w%d%d" % (a, u))

        def cast_x(h, a, engine):
            x_bf[h, a] = tile([P, HALF, PACK], BF16, "x_bf%d%d" % (h, a))
            copy(
                engine,
                x_bf[h, a][:].rearrange("p (c i) j -> p c j i", i=4),
                x_raw[h, a][:].rearrange("p j (c i) -> p c j i", i=4),
            )

        def quant_x(h, a):
            x_q[h, a] = quantize(x_bf[h, a][:].rearrange("p s j -> p (s j)"), HALF, "x%d%d" % (h, a))

        h_acc = [ps.tile([P, PACK, HALF], F32, name="h_acc%d" % h) for h in range(2)]

        def first_product(h, a):
            x_codes, x_plane = x_q[h, a]
            for t in range(PACK):
                w_codes, w_plane = w_q[a, t // 2]
                cols = slice(P * (t % 2), P * (t % 2 + 1))
                nc.tensor.matmul_mx(
                    out=h_acc[h][:, t, :],
                    lhsT=w_codes[:, cols].bitcast(FP8X4),
                    lhsT_scale=w_plane[:, cols],
                    rhs=x_codes[:].bitcast(FP8X4),
                    rhs_scale=x_plane[:],
                    start=(a == 0 and t == 0),
                    stop=(a == PASSES - 1 and t == PACK - 1),
                )

        h_bf = {}
        h_q = {}
        y_acc = {}
        y = {}

        def relu(h):
            h_bf[h] = tile([P, HALF, PACK], BF16, "h_bf%d" % h, "x_raw11" if h == 0 else None)
            nc.scalar.activation(out=h_bf[h][:], in_=h_acc[h][:].rearrange("p t s -> p s t"), func=ACT.Relu)

        def quant_h(h):
            h_q[h] = quantize(h_bf[h][:].rearrange("p s t -> p (s t)"), HALF, "h%d" % h)

        def second_product(h, c):
            h_codes, h_plane = h_q[h]
            y_acc[h, c] = ps.tile([P, HALF], F32, name="y_acc%d%d" % (h, c))
            nc.tensor.matmul_mx(
                out=y_acc[h, c][:],
                lhsT=w2_codes[c][:].bitcast(FP4X4),
                lhsT_scale=w2_plane[:, P * c : P * (c + 1)],
                rhs=h_codes[:].bitcast(FP8X4),
                rhs_scale=h_plane[:],
                start=True,
                stop=True,
            )

        def add_bias(h, c):
            y[h, c] = tile([P, HALF], F32, "y%d%d" % (h, c))
            nc.scalar.activation(out=y[h, c][:], in_=y_acc[h, c][:], func=ACT.Identity, bias=bias[:, c : c + 1])

        def scatter(h, c):
            window = pages[c][:].indirect(offsets[:, 8 * h : 8 * (h + 1)])
            nc.vector.tensor_tensor(window, y[h, c][:], weights[:, HALF * h : HALF * (h + 1)], MULT)

        for a in range(PASSES - 1):
            cast_w1(a, 0, 0, 1, "scalar")
            cast_w1(a, 1, 0, 1, "vector")
            quant_w1(a, 1)
            quant_w1(a, 0)
        for c in range(2):
            cast_w1(3, 0, c, 2, "scalar")
            cast_w1(3, 1, c, 2, "vector")
        quant_w1(3, 1)
        quant_w1(3, 0)
        for a in range(3):
            cast_x(0, a, "scalar")
        for a in range(2):
            quant_x(0, a)
            first_product(0, a)
        cast_x(0, 3, "vector")
        for a in range(2, 4):
            quant_x(0, a)
            first_product(0, a)
        cast_x(1, 0, "scalar")
        cast_x(1, 1, "scalar")
        relu(0)
        quant_x(1, 0)
        first_product(1, 0)
        cast_x(1, 2, "vector")
        quant_x(1, 1)
        first_product(1, 1)
        quant_x(1, 2)
        first_product(1, 2)
        cast_x(1, 3, "vector")
        quant_h(0)
        quant_x(1, 3)
        second_product(0, 0)
        first_product(1, 3)
        second_product(0, 1)
        add_bias(0, 0)
        relu(1)
        add_bias(0, 1)
        scatter(0, 0)
        quant_h(1)
        scatter(0, 1)
        for c in range(BLOCKS):
            second_product(1, c)
            add_bias(1, c)
        for c in range(BLOCKS):
            scatter(1, c)
            nc.sync.dma_start(out=out[P * c : P * (c + 1), :], in_=pages[c][:])
